import numpy as np
import ml_dtypes


def mxq(x, axis, fmt="e4m3"):
    dtype, down = {"e4m3": (ml_dtypes.float8_e4m3fn, 7), "e5m2": (ml_dtypes.float8_e5m2, 14)}[fmt]
    v = np.moveaxis(np.asarray(x, np.float32).astype(ml_dtypes.bfloat16).astype(np.float64), axis, -1)
    blocks = v.reshape(v.shape[:-1] + (-1, 32))
    amax = np.abs(blocks).max(-1, keepdims=True)
    byte = np.maximum(np.where(amax > 0, np.frexp(amax)[1] - 1 + 127, 0) - down, 1)
    scale = np.exp2(byte - 127.0)
    codes = (blocks / scale).astype(np.float32).astype(dtype).astype(np.float64)
    return np.moveaxis((codes * scale).reshape(v.shape), -1, axis)


WIDE = False


def mx_kscale(k):
    if not WIDE:
        return np.ones(k)
    levels = np.array([30, -30])
    if k % 512:
        return np.exp2(np.random.permutation(np.resize(levels, k // 32))).repeat(32)
    a = np.empty((k // 512, 16))
    for p in range(k // 512):
        a[p, :8] = np.random.permutation(np.resize(levels, 8))
        for g in range(8):
            far = levels[np.abs(levels - a[p, g]) >= 10]
            a[p, g + 8] = far[np.random.randint(len(far))]
    return np.exp2(a.ravel()).repeat(32)


def f64(x):
    return np.asarray(x).astype(np.float64)


def striped8(idx):
    return np.asarray(idx).reshape(8, -1, 16).transpose(0, 2, 1).reshape(128, -1).astype(np.uint16)


def unstriped8(offs):
    return offs.reshape(8, 16, -1).transpose(0, 2, 1).reshape(8, -1).astype(np.int64)


def pick8(x, idx, run):
    r = np.arange(len(x))
    return x[r[:, None], idx[r % (8 * run) // run]]


E2M1 = np.array([0.0, 0.5, 1.0, 1.5, 2.0, 3.0, 4.0, 6.0, -0.0, -0.5, -1.0, -1.5, -2.0, -3.0, -4.0, -6.0])


def pack_weight(w, fmt):
    k, n = w.shape
    w = f64(np.asarray(w, np.float32).astype(ml_dtypes.bfloat16)).reshape(k // 32, 32, n)
    amax = np.abs(w).max(1)
    if fmt == "e4m3":
        byte = np.frexp(amax)[1] - 1 + 127 - 7
    else:
        mant, ex = np.frexp(amax / 6.0)
        byte = np.where(mant > 0.5, ex, ex - 1) + 127
    byte = np.clip(np.where(amax > 0, byte, 1), 1, 254)
    scaled = (w * np.exp2(127.0 - byte)[:, None, :]).reshape(k, n).astype(np.float32)
    by_word = np.ascontiguousarray(scaled.reshape(k // 512, 128, 4, n).transpose(0, 1, 3, 2))
    if fmt == "e4m3":
        words = by_word.astype(ml_dtypes.float8_e4m3fn).view(np.uint8)
    else:
        c = by_word.astype(ml_dtypes.float4_e2m1fn).view(np.uint8) & 0xF
        words = (c[..., 0::2] | (c[..., 1::2] << 4)).reshape(k // 512, 128, 2 * n)
    return np.ascontiguousarray(words), np.ascontiguousarray(byte.astype(np.uint8).reshape(k // 512, 16, n))


def unpack_weight(words, scales, fmt):
    g, _, n = scales.shape
    words = np.ascontiguousarray(words).reshape(g, 128, n, -1)
    if fmt == "e4m3":
        vals = words.view(ml_dtypes.float8_e4m3fn).astype(np.float64)
    else:
        nib = np.empty((g, 128, n, 4), np.uint8)
        nib[..., 0::2] = words & 0xF
        nib[..., 1::2] = words >> 4
        vals = E2M1[nib]
    vals = vals * np.repeat(np.exp2(scales.astype(np.float64) - 127.0), 8, axis=1)[..., None]
    return vals.transpose(0, 1, 3, 2).reshape(g * 512, n)


def bf(x):
    return np.asarray(x, np.float32).astype(ml_dtypes.bfloat16)


def planes(Y):
    r, m = Y.shape
    b = f64(bf(Y)).reshape(r // 32, 32, m)
    amax = np.abs(b).max(1)
    byte = np.clip(np.where(amax > 0, np.frexp(amax)[1] - 1 + 127 - 7, 1), 1, 254)
    codes = (b * np.exp2(127.0 - byte)[:, None, :]).reshape(r, m).astype(np.float32).astype(ml_dtypes.float8_e4m3fn).view(np.uint8)
    words = codes.reshape(r // 512, 128, 4, m).transpose(0, 1, 3, 2)
    return np.ascontiguousarray(words), np.ascontiguousarray(byte.astype(np.uint8).reshape(r // 512, 16, m))


N, K, T, J = 512, 512, 1024, 512


def setup_inputs():
    n = np.random.standard_normal
    idx = np.stack([np.random.permutation(T)[:J] for _ in range(8)])
    fn = mx_kscale(N)
    wp = pack_weight(n((N, K)) * 1 / np.sqrt(N) * fn[:, None], "e4m3")
    return {
        "g": (n((N, T)) * np.exp(0.5 * n((1, T))) / fn[:, None]).astype(np.float32),
        "gm": (np.random.uniform(0.5, 2.0, (N, 1))).astype(np.float32),
        "w_words": wp[0],
        "w_scales": wp[1],
        "base": (1.0 * n((K, J))).astype(np.float32),
        "offs": striped8(idx),
    }


def reference(g, gm, w_words, w_scales, base, offs):
    idx = unstriped8(offs)
    wu = unpack_weight(w_words, w_scales, "e4m3")
    d = pick8(f64(g), idx, 64) * f64(gm)
    dq = mxq(d, 0, "e5m2")
    dx = wu.T @ dq
    y = dx + 0.5 * f64(base)
    words, scales = planes(y)
    return y, words, scales

@@ -1,0 +1,166 @@
+from contextlib import ExitStack
+
+import concourse.mybir as mybir
+
+N, K, T, J = 512, 512, 1024, 512
+FLOPS = 2 * N * K * J
+
+F32 = mybir.dt.float32
+BF16 = mybir.dt.bfloat16
+I32 = mybir.dt.int32
+U32 = mybir.dt.uint32
+U16 = mybir.dt.uint16
+U8 = mybir.dt.uint8
+E4M3 = mybir.dt.float8_e4m3fn_x4
+E5M2 = mybir.dt.float8_e5m2_x4
+MULT = mybir.AluOpType.mult
+ADD = mybir.AluOpType.add
+COPY = mybir.ActivationFunctionType.Copy
+
+P = 128
+PACK = 4
+HALF = J // 2
+QUART = J // 4
+
+
+def tile_list_head_token_grads_pl_kernel(tc, g, gm, w_words, w_scales, base, offs, out_0, out_1, out_2):
+    nc = tc.nc
+    with ExitStack() as ctx:
+        sb = ctx.enter_context(tc.tile_pool(name="sb", bufs=1))
+        ps = ctx.enter_context(tc.psum_pool(name="ps", bufs=1))
+
+        offsets = sb.tile([P, J // 16], U16, name="offsets")
+        gm_sb = sb.tile([P, PACK], F32, name="gm_sb")
+        g_rows = [sb.tile([P, T], F32, name=f"g_rows{t}", align_bytes=64) for t in range(PACK)]
+        ws_raw = sb.tile([P, K], U8, name="ws_raw", align_bytes=64)
+        ww_raw = sb.tile([P, K], U32, name="ww_raw", align_bytes=64)
+        base_sb = [sb.tile([P, PACK, HALF], F32, name=f"base_sb{h}", align_bytes=64) for h in range(2)]
+
+        g_dealt = g.rearrange("(p t) c -> t p c", t=PACK)
+        base_dealt = base.rearrange("(p t) j -> p t j", t=PACK)
+        y_dealt = out_0.rearrange("(p t) j -> p t j", t=PACK)
+
+        nc.vector.memset(ws_raw[:].bitcast(I32), 0)
+        nc.sync.dma_start(out=g_rows[0][:], in_=g_dealt[0])
+        nc.sync.dma_start(offsets[:], offs)
+        nc.scalar.dma_start(out=gm_sb[:], in_=gm.rearrange("(p t) o -> p (t o)", t=PACK))
+        for t in (1, 2):
+            nc.sync.dma_start(out=g_rows[t][:], in_=g_dealt[t])
+        for q in range(4):
+            nc.sync.dma_start(
+                out=ws_raw[32 * q : 32 * q + 4, :].bitcast(I32),
+                in_=w_scales[0, 4 * q : 4 * q + 4, :].bitcast(I32),
+            )
+        nc.sync.dma_start(out=g_rows[3][:], in_=g_dealt[3])
+        nc.sync.dma_start(
+            out=ww_raw[:].bitcast(I32), in_=w_words[0].rearrange("p c r -> p (c r)").bitcast(I32)
+        )
+        for h in range(2):
+            nc.sync.dma_start(out=base_sb[h][:], in_=base_dealt[:, :, h * HALF : (h + 1) * HALF])
+
+        ws = sb.tile([P, PACK, P], U8, name="ws", align_bytes=64)
+        pairs = [sb.tile([P, 2, HALF, 2], BF16, name=f"pairs{h}", align_bytes=64) for h in range(2)]
+        for t in range(PACK):
+            picked = [sb.tile([P, HALF], F32, name=f"picked{t}_{h}", align_bytes=64) for h in range(2)]
+            nc.vector.tensor_copy(out=picked[0][:], in_=g_rows[t][:].indirect(offsets[:, 0:16]))
+            nc.scalar.activation(out=picked[1][:], in_=g_rows[t][:].indirect(offsets[:, 16:32]), func=COPY)
+            for h in range(2):
+                if h == 1:
+                    nc.scalar.activation(
+                        out=pairs[h][:, t // 2, :, t % 2], in_=picked[h][:], func=COPY, scale=gm_sb[:, t : t + 1]
+                    )
+                else:
+                    nc.vector.tensor_scalar(
+                        out=pairs[h][:, t // 2, :, t % 2],
+                        in0=picked[h][:],
+                        scalar1=gm_sb[:, t : t + 1],
+                        scalar2=None,
+                        op0=MULT,
+                    )
+            if t == 2:
+                nc.vector.tensor_copy(out=ws[:], in_=ws_raw[:].rearrange("p (m t) -> p t m", t=PACK))
+
+        ww = [sb.tile([P, 2, P], U32, name=f"ww{u}", align_bytes=64) for u in range(2)]
+        ww_dealt = ww_raw[:].bitcast(I32).rearrange("p (m t) -> p t m", t=PACK)
+        d_bf = [sb.tile([P, QUART * PACK], BF16, name=f"d_bf{c}", align_bytes=64) for c in range(4)]
+        d_words = [sb.tile([P, QUART], U32, name=f"d_words{c}", align_bytes=64) for c in range(4)]
+        d_scales = [sb.tile([P, QUART], U8, name=f"d_scales{c}", align_bytes=64) for c in range(4)]
+
+        def weave(c):
+            pair_words = pairs[c // 2][:].rearrange("p u j e -> p u (j e)").bitcast(F32)
+            c0 = (c % 2) * QUART
+            copy = nc.vector.tensor_copy if c < 2 else nc.scalar.copy
+            copy(
+                out=d_bf[c][:].bitcast(F32).rearrange("p (j u) -> p j u", u=2),
+                in_=pair_words[:, :, c0 : c0 + QUART].rearrange("p u j -> p j u"),
+            )
+
+        def deal(u):
+            nc.vector.tensor_copy(out=ww[u][:].bitcast(I32), in_=ww_dealt[:, 2 * u : 2 * u + 2, :])
+
+        def quant(c):
+            nc.vector.quantize_mx(out=d_words[c][:].bitcast(E5M2), scales=d_scales[c][:], in_=d_bf[c][:])
+
+        deal(0)
+        weave(0)
+        weave(1)
+        quant(0)
+        deal(1)
+        quant(1)
+        weave(2)
+        weave(3)
+        quant(2)
+        quant(3)
+
+        y_sb = [sb.tile([P, PACK, QUART], F32, name=f"y_sb{c}", align_bytes=64) for c in range(4)]
+        y_bf = []
+        for c in range(4):
+            h, c0 = c // 2, (c % 2) * QUART
+            acc = ps.tile([P, PACK, QUART], F32, name=f"acc{c}")
+            for t in range(PACK):
+                nc.tensor.matmul_mx(
+                    out=acc[:, t, :],
+                    lhsT=ww[t // 2][:, t % 2, :].bitcast(E4M3),
+                    lhsT_scale=ws[:, t, :],
+                    rhs=d_words[c][:].bitcast(E5M2),
+                    rhs_scale=d_scales[c][:],
+                    start=True,
+                    stop=True,
+                )
+            yb = sb.tile([P, QUART, PACK], BF16, name=f"y_bf{c}", align_bytes=64)
+            step = QUART // 2 if c == 3 else QUART
+            for j0 in range(0, QUART, step):
+                nc.vector.scalar_tensor_tensor(
+                    out=y_sb[c][:, :, j0 : j0 + step],
+                    in0=base_sb[h][:, :, c0 + j0 : c0 + j0 + step],
+                    scalar=0.5,
+                    in1=acc[:, :, j0 : j0 + step],
+                    op0=MULT,
+                    op1=ADD,
+                )
+                nc.scalar.copy(
+                    out=yb[:, j0 : j0 + step, :].rearrange("p (a i) t -> p a t i", i=4),
+                    in_=y_sb[c][:, :, j0 : j0 + step].rearrange("p t (a i) -> p a t i", i=4),
+                )
+            y_bf.append(yb)
+            nc.sync.dma_start(out=y_dealt[:, :, c * QUART : (c + 1) * QUART], in_=y_sb[c][:])
+
+        y_words = sb.tile([P, J], U32, name="y_words", align_bytes=64)
+        y_scales = sb.tile([P, J], U8, name="y_scales", align_bytes=64)
+        words_out = out_1[0].rearrange("p c r -> p (c r)").bitcast(I32)
+        for c in range(4):
+            cols = slice(c * QUART, (c + 1) * QUART)
+            nc.vector.quantize_mx(
+                out=y_words[:, cols].bitcast(E4M3),
+                scales=y_scales[:, cols],
+                in_=y_bf[c][:].rearrange("p j t -> p (j t)"),
+            )
+            if c % 2 == 1:
+                half = slice((c - 1) * QUART, (c + 1) * QUART)
+                nc.sync.dma_start(out=words_out[:, half], in_=y_words[:, half].bitcast(I32))
+        for q in range(4):
+            queue = nc.scalar if q % 2 == 0 else nc.sync
+            queue.dma_start(
+                out=out_2[0, 4 * q : 4 * q + 4, :].bitcast(I32),
+                in_=y_scales[32 * q : 32 * q + 4, :].bitcast(I32),
+            )

@@ -44,6 +44,10 @@ def tile_list_head_token_grads_pl_kernel(tc, g, gm, w_words, w_scales, base, off
         nc.sync.dma_start(out=g_rows[0][:], in_=g_dealt[0])
         nc.sync.dma_start(offsets[:], offs)
         nc.scalar.dma_start(out=gm_sb[:], in_=gm.rearrange("(p t) o -> p (t o)", t=PACK))
+        warm = sb.tile([P, 8], F32, name="warm")
+        warm2 = sb.tile([P, 8], F32, name="warm2")
+        nc.gpsimd.memset(warm[:], 0.0)
+        nc.scalar.activation(out=warm2[:], in_=warm[:], func=COPY)
         for t in (1, 2):
             nc.sync.dma_start(out=g_rows[t][:], in_=g_dealt[t])
         for q in range(4):

@@ -44,10 +44,6 @@ def tile_list_head_token_grads_pl_kernel(tc, g, gm, w_words, w_scales, base, off
         nc.sync.dma_start(out=g_rows[0][:], in_=g_dealt[0])
         nc.sync.dma_start(offsets[:], offs)
         nc.scalar.dma_start(out=gm_sb[:], in_=gm.rearrange("(p t) o -> p (t o)", t=PACK))
-        warm = sb.tile([P, 8], F32, name="warm")
-        warm2 = sb.tile([P, 8], F32, name="warm2")
-        nc.gpsimd.memset(warm[:], 0.0)
-        nc.scalar.activation(out=warm2[:], in_=warm[:], func=COPY)
         for t in (1, 2):
             nc.sync.dma_start(out=g_rows[t][:], in_=g_dealt[t])
         for q in range(4):
@@ -66,88 +62,81 @@ def tile_list_head_token_grads_pl_kernel(tc, g, gm, w_words, w_scales, base, off
         pairs = [sb.tile([P, 2, HALF, 2], BF16, name=f"pairs{h}", align_bytes=64) for h in range(2)]
         for t in range(PACK):
             picked = [sb.tile([P, HALF], F32, name=f"picked{t}_{h}", align_bytes=64) for h in range(2)]
+            factor = gm_sb[:, t : t + 1]
             nc.vector.tensor_copy(out=picked[0][:], in_=g_rows[t][:].indirect(offsets[:, 0:16]))
             nc.scalar.activation(out=picked[1][:], in_=g_rows[t][:].indirect(offsets[:, 16:32]), func=COPY)
-            for h in range(2):
-                if h == 1:
-                    nc.scalar.activation(
-                        out=pairs[h][:, t // 2, :, t % 2], in_=picked[h][:], func=COPY, scale=gm_sb[:, t : t + 1]
-                    )
-                else:
-                    nc.vector.tensor_scalar(
-                        out=pairs[h][:, t // 2, :, t % 2],
-                        in0=picked[h][:],
-                        scalar1=gm_sb[:, t : t + 1],
-                        scalar2=None,
-                        op0=MULT,
-                    )
+            step = QUART if t == PACK - 1 else HALF
+            for j0 in range(0, HALF, step):
+                nc.vector.tensor_scalar(
+                    out=pairs[0][:, t // 2, j0 : j0 + step, t % 2],
+                    in0=picked[0][:, j0 : j0 + step],
+                    scalar1=factor,
+                    scalar2=None,
+                    op0=MULT,
+                )
+            nc.scalar.activation(out=pairs[1][:, t // 2, :, t % 2], in_=picked[1][:], func=COPY, scale=factor)
             if t == 2:
                 nc.vector.tensor_copy(out=ws[:], in_=ws_raw[:].rearrange("p (m t) -> p t m", t=PACK))
 
         ww = [sb.tile([P, 2, P], U32, name=f"ww{u}", align_bytes=64) for u in range(2)]
-        ww_dealt = ww_raw[:].bitcast(I32).rearrange("p (m t) -> p t m", t=PACK)
-        d_bf = [sb.tile([P, QUART * PACK], BF16, name=f"d_bf{c}", align_bytes=64) for c in range(4)]
-        d_words = [sb.tile([P, QUART], U32, name=f"d_words{c}", align_bytes=64) for c in range(4)]
-        d_scales = [sb.tile([P, QUART], U8, name=f"d_scales{c}", align_bytes=64) for c in range(4)]
+        ww_dealt = ww_raw[:].rearrange("p (m t) -> p t m", t=PACK)
+        for u in range(2):
+            nc.scalar.copy(out=ww[u][:], in_=ww_dealt[:, 2 * u : 2 * u + 2, :])
 
-        def weave(c):
-            pair_words = pairs[c // 2][:].rearrange("p u j e -> p u (j e)").bitcast(F32)
+        d_words = [sb.tile([P, HALF], U32, name=f"d_words{h}", align_bytes=64) for h in range(2)]
+        d_scales = [sb.tile([P, HALF], U8, name=f"d_scales{h}", align_bytes=64) for h in range(2)]
+        for h in range(2):
+            pair_words = pairs[h][:].rearrange("p u j e -> p u (j e)").bitcast(F32)
+            d_bf = [sb.tile([P, QUART * PACK], BF16, name=f"d_bf{h}_{c}", align_bytes=64) for c in range(2)]
+            for c in range(2):
+                nc.vector.tensor_copy(
+                    out=d_bf[c][:].bitcast(F32).rearrange("p (j u) -> p j u", u=2),
+                    in_=pair_words[:, :, c * QUART : (c + 1) * QUART].rearrange("p u j -> p j u"),
+                )
+            for c in range(2):
+                cols = slice(c * QUART, (c + 1) * QUART)
+                nc.vector.quantize_mx(
+                    out=d_words[h][:, cols].bitcast(E5M2), scales=d_scales[h][:, cols], in_=d_bf[c][:]
+                )
+
+        y_sb = [sb.tile([P, PACK, HALF], F32, name=f"y_sb{h}", align_bytes=64) for h in range(2)]
+        y_bf = [sb.tile([P, QUART, PACK], BF16, name=f"y_bf{c}", align_bytes=64) for c in range(4)]
+
+        def round_quarter(c, copy):
             c0 = (c % 2) * QUART
-            copy = nc.vector.tensor_copy if c < 2 else nc.scalar.copy
             copy(
-                out=d_bf[c][:].bitcast(F32).rearrange("p (j u) -> p j u", u=2),
-                in_=pair_words[:, :, c0 : c0 + QUART].rearrange("p u j -> p j u"),
+                out=y_bf[c][:].rearrange("p (a i) t -> p a t i", i=4),
+                in_=y_sb[c // 2][:, :, c0 : c0 + QUART].rearrange("p t (a i) -> p a t i", i=4),
             )
 
-        def deal(u):
-            nc.vector.tensor_copy(out=ww[u][:].bitcast(I32), in_=ww_dealt[:, 2 * u : 2 * u + 2, :])
-
-        def quant(c):
-            nc.vector.quantize_mx(out=d_words[c][:].bitcast(E5M2), scales=d_scales[c][:], in_=d_bf[c][:])
-
-        deal(0)
-        weave(0)
-        weave(1)
-        quant(0)
-        deal(1)
-        quant(1)
-        weave(2)
-        weave(3)
-        quant(2)
-        quant(3)
-
-        y_sb = [sb.tile([P, PACK, QUART], F32, name=f"y_sb{c}", align_bytes=64) for c in range(4)]
-        y_bf = []
-        for c in range(4):
-            h, c0 = c // 2, (c % 2) * QUART
-            acc = ps.tile([P, PACK, QUART], F32, name=f"acc{c}")
-            for t in range(PACK):
+        for h, t0, t1 in ((0, 0, 1), (0, 1, 2), (0, 2, 4), (1, 0, 2), (1, 2, 4)):
+            acc = ps.tile([P, t1 - t0, HALF], F32, name=f"acc{h}_{t0}")
+            for t in range(t0, t1):
                 nc.tensor.matmul_mx(
-                    out=acc[:, t, :],
+                    out=acc[:, t - t0, :],
                     lhsT=ww[t // 2][:, t % 2, :].bitcast(E4M3),
                     lhsT_scale=ws[:, t, :],
-                    rhs=d_words[c][:].bitcast(E5M2),
-                    rhs_scale=d_scales[c][:],
+                    rhs=d_words[h][:].bitcast(E5M2),
+                    rhs_scale=d_scales[h][:],
                     start=True,
                     stop=True,
                 )
-            yb = sb.tile([P, QUART, PACK], BF16, name=f"y_bf{c}", align_bytes=64)
-            step = QUART // 2 if c == 3 else QUART
-            for j0 in range(0, QUART, step):
+            last = h == 1 and t1 == PACK
+            step = QUART if last else HALF
+            for j0 in range(0, HALF, step):
                 nc.vector.scalar_tensor_tensor(
-                    out=y_sb[c][:, :, j0 : j0 + step],
-                    in0=base_sb[h][:, :, c0 + j0 : c0 + j0 + step],
+                    out=y_sb[h][:, t0:t1, j0 : j0 + step],
+                    in0=base_sb[h][:, t0:t1, j0 : j0 + step],
                     scalar=0.5,
                     in1=acc[:, :, j0 : j0 + step],
                     op0=MULT,
                     op1=ADD,
                 )
-                nc.scalar.copy(
-                    out=yb[:, j0 : j0 + step, :].rearrange("p (a i) t -> p a t i", i=4),
-                    in_=y_sb[c][:, :, j0 : j0 + step].rearrange("p t (a i) -> p a t i", i=4),
-                )
-            y_bf.append(yb)
-            nc.sync.dma_start(out=y_dealt[:, :, c * QUART : (c + 1) * QUART], in_=y_sb[c][:])
+            nc.sync.dma_start(out=y_dealt[:, t0:t1, h * HALF : (h + 1) * HALF], in_=y_sb[h][:, t0:t1, :])
+            if h == 0 and t1 == PACK:
+                round_quarter(0, nc.scalar.copy)
+                round_quarter(1, nc.scalar.copy)
+        round_quarter(2, nc.scalar.copy)
 
         y_words = sb.tile([P, J], U32, name="y_words", align_bytes=64)
         y_scales = sb.tile([P, J], U8, name="y_scales", align_bytes=64)
@@ -159,6 +148,8 @@ def tile_list_head_token_grads_pl_kernel(tc, g, gm, w_words, w_scales, base, off
                 scales=y_scales[:, cols],
                 in_=y_bf[c][:].rearrange("p j t -> p (j t)"),
             )
+            if c == 0:
+                round_quarter(3, nc.vector.tensor_copy)
             if c % 2 == 1:
                 half = slice((c - 1) * QUART, (c + 1) * QUART)
                 nc.sync.dma_start(out=words_out[:, half], in_=y_words[:, half].bitcast(I32))

@@ -44,6 +44,10 @@ def tile_list_head_token_grads_pl_kernel(tc, g, gm, w_words, w_scales, base, off
         nc.sync.dma_start(out=g_rows[0][:], in_=g_dealt[0])
         nc.sync.dma_start(offsets[:], offs)
         nc.scalar.dma_start(out=gm_sb[:], in_=gm.rearrange("(p t) o -> p (t o)", t=PACK))
+        warm = sb.tile([P, 8], F32, name="warm")
+        warm2 = sb.tile([P, 8], F32, name="warm2")
+        nc.gpsimd.memset(warm[:], 0.0)
+        nc.scalar.activation(out=warm2[:], in_=warm[:], func=COPY)
         for t in (1, 2):
             nc.sync.dma_start(out=g_rows[t][:], in_=g_dealt[t])
         for q in range(4):
@@ -63,8 +67,8 @@ def tile_list_head_token_grads_pl_kernel(tc, g, gm, w_words, w_scales, base, off
         for t in range(PACK):
             picked = [sb.tile([P, HALF], F32, name=f"picked{t}_{h}", align_bytes=64) for h in range(2)]
             factor = gm_sb[:, t : t + 1]
-            nc.vector.tensor_copy(out=picked[0][:], in_=g_rows[t][:].indirect(offsets[:, 0:16]))
-            nc.scalar.activation(out=picked[1][:], in_=g_rows[t][:].indirect(offsets[:, 16:32]), func=COPY)
+            nc.scalar.activation(out=picked[0][:], in_=g_rows[t][:].indirect(offsets[:, 0:16]), func=COPY)
+            nc.vector.tensor_copy(out=picked[1][:], in_=g_rows[t][:].indirect(offsets[:, 16:32]))
             step = QUART if t == PACK - 1 else HALF
             for j0 in range(0, HALF, step):
                 nc.vector.tensor_scalar(
@@ -79,64 +83,56 @@ def tile_list_head_token_grads_pl_kernel(tc, g, gm, w_words, w_scales, base, off
                 nc.vector.tensor_copy(out=ws[:], in_=ws_raw[:].rearrange("p (m t) -> p t m", t=PACK))
 
         ww = [sb.tile([P, 2, P], U32, name=f"ww{u}", align_bytes=64) for u in range(2)]
-        ww_dealt = ww_raw[:].rearrange("p (m t) -> p t m", t=PACK)
+        ww_by_m = ww_raw[:].rearrange("p (m t) -> p m t", t=PACK)
         for u in range(2):
-            nc.scalar.copy(out=ww[u][:], in_=ww_dealt[:, 2 * u : 2 * u + 2, :])
+            nc.scalar.copy(out=ww[u][:].rearrange("p t m -> p m t"), in_=ww_by_m[:, :, 2 * u : 2 * u + 2])
 
-        d_words = [sb.tile([P, HALF], U32, name=f"d_words{h}", align_bytes=64) for h in range(2)]
-        d_scales = [sb.tile([P, HALF], U8, name=f"d_scales{h}", align_bytes=64) for h in range(2)]
+        d_bf = [sb.tile([P, QUART * PACK], BF16, name=f"d_bf{c}", align_bytes=64) for c in range(4)]
+        d_words = [sb.tile([P, QUART], U32, name=f"d_words{c}", align_bytes=64) for c in range(4)]
+        d_scales = [sb.tile([P, QUART], U8, name=f"d_scales{c}", align_bytes=64) for c in range(4)]
         for h in range(2):
             pair_words = pairs[h][:].rearrange("p u j e -> p u (j e)").bitcast(F32)
-            d_bf = [sb.tile([P, QUART * PACK], BF16, name=f"d_bf{h}_{c}", align_bytes=64) for c in range(2)]
-            for c in range(2):
+            for c in (2 * h, 2 * h + 1):
+                c0 = (c % 2) * QUART
                 nc.vector.tensor_copy(
                     out=d_bf[c][:].bitcast(F32).rearrange("p (j u) -> p j u", u=2),
-                    in_=pair_words[:, :, c * QUART : (c + 1) * QUART].rearrange("p u j -> p j u"),
+                    in_=pair_words[:, :, c0 : c0 + QUART].rearrange("p u j -> p j u"),
                 )
-            for c in range(2):
-                cols = slice(c * QUART, (c + 1) * QUART)
-                nc.vector.quantize_mx(
-                    out=d_words[h][:, cols].bitcast(E5M2), scales=d_scales[h][:, cols], in_=d_bf[c][:]
-                )
+            for c in (2 * h, 2 * h + 1):
+                nc.vector.quantize_mx(out=d_words[c][:].bitcast(E5M2), scales=d_scales[c][:], in_=d_bf[c][:])
 
-        y_sb = [sb.tile([P, PACK, HALF], F32, name=f"y_sb{h}", align_bytes=64) for h in range(2)]
-        y_bf = [sb.tile([P, QUART, PACK], BF16, name=f"y_bf{c}", align_bytes=64) for c in range(4)]
-
-        def round_quarter(c, copy):
-            c0 = (c % 2) * QUART
-            copy(
-                out=y_bf[c][:].rearrange("p (a i) t -> p a t i", i=4),
-                in_=y_sb[c // 2][:, :, c0 : c0 + QUART].rearrange("p t (a i) -> p a t i", i=4),
-            )
-
-        for h, t0, t1 in ((0, 0, 1), (0, 1, 2), (0, 2, 4), (1, 0, 2), (1, 2, 4)):
-            acc = ps.tile([P, t1 - t0, HALF], F32, name=f"acc{h}_{t0}")
-            for t in range(t0, t1):
+        y_sb = [sb.tile([P, PACK, QUART], F32, name=f"y_sb{c}", align_bytes=64) for c in range(4)]
+        y_bf = []
+        for c in range(4):
+            h, c0 = c // 2, (c % 2) * QUART
+            acc = ps.tile([P, PACK, QUART], F32, name=f"acc{c}")
+            for t in range(PACK):
                 nc.tensor.matmul_mx(
-                    out=acc[:, t - t0, :],
+                    out=acc[:, t, :],
                     lhsT=ww[t // 2][:, t % 2, :].bitcast(E4M3),
                     lhsT_scale=ws[:, t, :],
-                    rhs=d_words[h][:].bitcast(E5M2),
-                    rhs_scale=d_scales[h][:],
+                    rhs=d_words[c][:].bitcast(E5M2),
+                    rhs_scale=d_scales[c][:],
                     start=True,
                     stop=True,
                 )
-            last = h == 1 and t1 == PACK
-            step = QUART if last else HALF
-            for j0 in range(0, HALF, step):
+            yb = sb.tile([P, QUART, PACK], BF16, name=f"y_bf{c}", align_bytes=64)
+            step = QUART // 2 if c == 3 else QUART
+            for j0 in range(0, QUART, step):
                 nc.vector.scalar_tensor_tensor(
-                    out=y_sb[h][:, t0:t1, j0 : j0 + step],
-                    in0=base_sb[h][:, t0:t1, j0 : j0 + step],
+                    out=y_sb[c][:, :, j0 : j0 + step],
+                    in0=base_sb[h][:, :, c0 + j0 : c0 + j0 + step],
                     scalar=0.5,
                     in1=acc[:, :, j0 : j0 + step],
                     op0=MULT,
                     op1=ADD,
                 )
-            nc.sync.dma_start(out=y_dealt[:, t0:t1, h * HALF : (h + 1) * HALF], in_=y_sb[h][:, t0:t1, :])
-            if h == 0 and t1 == PACK:
-                round_quarter(0, nc.scalar.copy)
-                round_quarter(1, nc.scalar.copy)
-        round_quarter(2, nc.scalar.copy)
+                nc.scalar.copy(
+                    out=yb[:, j0 : j0 + step, :].rearrange("p (a i) t -> p a t i", i=4),
+                    in_=y_sb[c][:, :, j0 : j0 + step].rearrange("p t (a i) -> p a t i", i=4),
+                )
+            y_bf.append(yb)
+            nc.sync.dma_start(out=y_dealt[:, :, c * QUART : (c + 1) * QUART], in_=y_sb[c][:])
 
         y_words = sb.tile([P, J], U32, name="y_words", align_bytes=64)
         y_scales = sb.tile([P, J], U8, name="y_scales", align_bytes=64)
@@ -148,8 +144,6 @@ def tile_list_head_token_grads_pl_kernel(tc, g, gm, w_words, w_scales, base, off
                 scales=y_scales[:, cols],
                 in_=y_bf[c][:].rearrange("p j t -> p (j t)"),
             )
-            if c == 0:
-                round_quarter(3, nc.vector.tensor_copy)
             if c % 2 == 1:
                 half = slice((c - 1) * QUART, (c + 1) * QUART)
                 nc.sync.dma_start(out=words_out[:, half], in_=y_words[:, half].bitcast(I32))

from contextlib import ExitStack

import concourse.mybir as mybir

N, K, T, J = 512, 512, 1024, 512
FLOPS = 2 * N * K * J

F32 = mybir.dt.float32
BF16 = mybir.dt.bfloat16
I32 = mybir.dt.int32
U32 = mybir.dt.uint32
U16 = mybir.dt.uint16
U8 = mybir.dt.uint8
E4M3 = mybir.dt.float8_e4m3fn_x4
E5M2 = mybir.dt.float8_e5m2_x4
MULT = mybir.AluOpType.mult
ADD = mybir.AluOpType.add
COPY = mybir.ActivationFunctionType.Copy

P = 128
PACK = 4
HALF = J // 2
QUART = J // 4


def tile_list_head_token_grads_pl_kernel(tc, g, gm, w_words, w_scales, base, offs, out_0, out_1, out_2):
    nc = tc.nc
    with ExitStack() as ctx:
        sb = ctx.enter_context(tc.tile_pool(name="sb", bufs=1))
        ps = ctx.enter_context(tc.psum_pool(name="ps", bufs=1))

        offsets = sb.tile([P, J // 16], U16, name="offsets")
        gm_sb = sb.tile([P, PACK], F32, name="gm_sb")
        g_rows = [sb.tile([P, T], F32, name=f"g_rows{t}", align_bytes=64) for t in range(PACK)]
        ws_raw = sb.tile([P, K], U8, name="ws_raw", align_bytes=64)
        ww_raw = sb.tile([P, K], U32, name="ww_raw", align_bytes=64)
        base_sb = [sb.tile([P, PACK, HALF], F32, name=f"base_sb{h}", align_bytes=64) for h in range(2)]

        g_dealt = g.rearrange("(p t) c -> t p c", t=PACK)
        base_dealt = base.rearrange("(p t) j -> p t j", t=PACK)
        y_dealt = out_0.rearrange("(p t) j -> p t j", t=PACK)

        nc.vector.memset(ws_raw[:].bitcast(I32), 0)
        nc.sync.dma_start(out=g_rows[0][:], in_=g_dealt[0])
        nc.sync.dma_start(offsets[:], offs)
        nc.scalar.dma_start(out=gm_sb[:], in_=gm.rearrange("(p t) o -> p (t o)", t=PACK))
        warm = sb.tile([P, 8], F32, name="warm")
        warm2 = sb.tile([P, 8], F32, name="warm2")
        nc.gpsimd.memset(warm[:], 0.0)
        nc.scalar.activation(out=warm2[:], in_=warm[:], func=COPY)
        for t in (1, 2):
            nc.sync.dma_start(out=g_rows[t][:], in_=g_dealt[t])
        for q in range(4):
            nc.sync.dma_start(
                out=ws_raw[32 * q : 32 * q + 4, :].bitcast(I32),
                in_=w_scales[0, 4 * q : 4 * q + 4, :].bitcast(I32),
            )
        nc.sync.dma_start(out=g_rows[3][:], in_=g_dealt[3])
        nc.sync.dma_start(
            out=ww_raw[:].bitcast(I32), in_=w_words[0].rearrange("p c r -> p (c r)").bitcast(I32)
        )
        for h in range(2):
            nc.sync.dma_start(out=base_sb[h][:], in_=base_dealt[:, :, h * HALF : (h + 1) * HALF])

        ws = sb.tile([P, PACK, P], U8, name="ws", align_bytes=64)
        pairs = [sb.tile([P, 2, HALF, 2], BF16, name=f"pairs{h}", align_bytes=64) for h in range(2)]
        for t in range(PACK):
            picked = [sb.tile([P, HALF], F32, name=f"picked{t}_{h}", align_bytes=64) for h in range(2)]
            factor = gm_sb[:, t : t + 1]
            nc.scalar.activation(out=picked[0][:], in_=g_rows[t][:].indirect(offsets[:, 0:16]), func=COPY)
            nc.vector.tensor_copy(out=picked[1][:], in_=g_rows[t][:].indirect(offsets[:, 16:32]))
            step = QUART if t == PACK - 1 else HALF
            for j0 in range(0, HALF, step):
                nc.vector.tensor_scalar(
                    out=pairs[0][:, t // 2, j0 : j0 + step, t % 2],
                    in0=picked[0][:, j0 : j0 + step],
                    scalar1=factor,
                    scalar2=None,
                    op0=MULT,
                )
            nc.scalar.activation(out=pairs[1][:, t // 2, :, t % 2], in_=picked[1][:], func=COPY, scale=factor)
            if t == 2:
                nc.vector.tensor_copy(out=ws[:], in_=ws_raw[:].rearrange("p (m t) -> p t m", t=PACK))

        ww = [sb.tile([P, 2, P], U32, name=f"ww{u}", align_bytes=64) for u in range(2)]
        ww_by_m = ww_raw[:].rearrange("p (m t) -> p m t", t=PACK)
        for u in range(2):
            nc.scalar.copy(out=ww[u][:].rearrange("p t m -> p m t"), in_=ww_by_m[:, :, 2 * u : 2 * u + 2])

        d_bf = [sb.tile([P, QUART * PACK], BF16, name=f"d_bf{c}", align_bytes=64) for c in range(4)]
        d_words = [sb.tile([P, QUART], U32, name=f"d_words{c}", align_bytes=64) for c in range(4)]
        d_scales = [sb.tile([P, QUART], U8, name=f"d_scales{c}", align_bytes=64) for c in range(4)]
        for h in range(2):
            pair_words = pairs[h][:].rearrange("p u j e -> p u (j e)").bitcast(F32)
            for c in (2 * h, 2 * h + 1):
                c0 = (c % 2) * QUART
                nc.vector.tensor_copy(
                    out=d_bf[c][:].bitcast(F32).rearrange("p (j u) -> p j u", u=2),
                    in_=pair_words[:, :, c0 : c0 + QUART].rearrange("p u j -> p j u"),
                )
            for c in (2 * h, 2 * h + 1):
                nc.vector.quantize_mx(out=d_words[c][:].bitcast(E5M2), scales=d_scales[c][:], in_=d_bf[c][:])

        y_sb = [sb.tile([P, PACK, QUART], F32, name=f"y_sb{c}", align_bytes=64) for c in range(4)]
        y_bf = []
        for c in range(4):
            h, c0 = c // 2, (c % 2) * QUART
            acc = ps.tile([P, PACK, QUART], F32, name=f"acc{c}")
            for t in range(PACK):
                nc.tensor.matmul_mx(
                    out=acc[:, t, :],
                    lhsT=ww[t // 2][:, t % 2, :].bitcast(E4M3),
                    lhsT_scale=ws[:, t, :],
                    rhs=d_words[c][:].bitcast(E5M2),
                    rhs_scale=d_scales[c][:],
                    start=True,
                    stop=True,
                )
            yb = sb.tile([P, QUART, PACK], BF16, name=f"y_bf{c}", align_bytes=64)
            step = QUART // 2 if c == 3 else QUART
            for j0 in range(0, QUART, step):
                nc.vector.scalar_tensor_tensor(
                    out=y_sb[c][:, :, j0 : j0 + step],
                    in0=base_sb[h][:, :, c0 + j0 : c0 + j0 + step],
                    scalar=0.5,
                    in1=acc[:, :, j0 : j0 + step],
                    op0=MULT,
                    op1=ADD,
                )
                nc.scalar.copy(
                    out=yb[:, j0 : j0 + step, :].rearrange("p (a i) t -> p a t i", i=4),
                    in_=y_sb[c][:, :, j0 : j0 + step].rearrange("p t (a i) -> p a t i", i=4),
                )
            y_bf.append(yb)
            nc.sync.dma_start(out=y_dealt[:, :, c * QUART : (c + 1) * QUART], in_=y_sb[c][:])

        y_words = sb.tile([P, J], U32, name="y_words", align_bytes=64)
        y_scales = sb.tile([P, J], U8, name="y_scales", align_bytes=64)
        words_out = out_1[0].rearrange("p c r -> p (c r)").bitcast(I32)
        for c in range(4):
            cols = slice(c * QUART, (c + 1) * QUART)
            nc.vector.quantize_mx(
                out=y_words[:, cols].bitcast(E4M3),
                scales=y_scales[:, cols],
                in_=y_bf[c][:].rearrange("p j t -> p (j t)"),
            )
            if c % 2 == 1:
                half = slice((c - 1) * QUART, (c + 1) * QUART)
                nc.sync.dma_start(out=words_out[:, half], in_=y_words[:, half].bitcast(I32))
        for q in range(4):
            queue = nc.scalar if q % 2 == 0 else nc.sync
            queue.dma_start(
                out=out_2[0, 4 * q : 4 * q + 4, :].bitcast(I32),
                in_=y_scales[32 * q : 32 * q + 4, :].bitcast(I32),
            )
